import numpy as np
import ml_dtypes


def mxq(x, axis, fmt="e4m3"):
    dtype, down = {"e4m3": (ml_dtypes.float8_e4m3fn, 7), "e5m2": (ml_dtypes.float8_e5m2, 14)}[fmt]
    v = np.moveaxis(np.asarray(x, np.float32).astype(ml_dtypes.bfloat16).astype(np.float64), axis, -1)
    blocks = v.reshape(v.shape[:-1] + (-1, 32))
    amax = np.abs(blocks).max(-1, keepdims=True)
    byte = np.maximum(np.where(amax > 0, np.frexp(amax)[1] - 1 + 127, 0) - down, 1)
    scale = np.exp2(byte - 127.0)
    codes = (blocks / scale).astype(np.float32).astype(dtype).astype(np.float64)
    return np.moveaxis((codes * scale).reshape(v.shape), -1, axis)


WIDE = False


def mx_kscale(k):
    if not WIDE:
        return np.ones(k)
    levels = np.array([10, -10, 5, -5, 0])
    if k % 512:
        return np.exp2(np.random.permutation(np.resize(levels, k // 32))).repeat(32)
    a = np.empty((k // 512, 16))
    for p in range(k // 512):
        a[p, :8] = np.random.permutation(np.resize(levels, 8))
        for g in range(8):
            far = levels[np.abs(levels - a[p, g]) >= 10]
            a[p, g + 8] = far[np.random.randint(len(far))]
    return np.exp2(a.ravel()).repeat(32)


def f64(x):
    return np.asarray(x).astype(np.float64)


def striped8(idx):
    return np.asarray(idx).reshape(8, -1, 16).transpose(0, 2, 1).reshape(128, -1).astype(np.uint16)


def unstriped8(offs):
    return offs.reshape(8, 16, -1).transpose(0, 2, 1).reshape(8, -1).astype(np.int64)


def pick8(x, idx, run):
    r = np.arange(len(x))
    return x[r[:, None], idx[r % (8 * run) // run]]


E2M1 = np.array([0.0, 0.5, 1.0, 1.5, 2.0, 3.0, 4.0, 6.0, -0.0, -0.5, -1.0, -1.5, -2.0, -3.0, -4.0, -6.0])


def pack_weight(w, fmt):
    k, n = w.shape
    w = f64(np.asarray(w, np.float32).astype(ml_dtypes.bfloat16)).reshape(k // 32, 32, n)
    amax = np.abs(w).max(1)
    if fmt == "e4m3":
        byte = np.frexp(amax)[1] - 1 + 127 - 7
    else:
        mant, ex = np.frexp(amax / 6.0)
        byte = np.where(mant > 0.5, ex, ex - 1) + 127
    byte = np.clip(np.where(amax > 0, byte, 1), 1, 254)
    scaled = (w * np.exp2(127.0 - byte)[:, None, :]).reshape(k, n).astype(np.float32)
    by_word = np.ascontiguousarray(scaled.reshape(k // 512, 128, 4, n).transpose(0, 1, 3, 2))
    if fmt == "e4m3":
        words = by_word.astype(ml_dtypes.float8_e4m3fn).view(np.uint8)
    else:
        c = by_word.astype(ml_dtypes.float4_e2m1fn).view(np.uint8) & 0xF
        words = (c[..., 0::2] | (c[..., 1::2] << 4)).reshape(k // 512, 128, 2 * n)
    return np.ascontiguousarray(words), np.ascontiguousarray(byte.astype(np.uint8).reshape(k // 512, 16, n))


def unpack_weight(words, scales, fmt):
    g, _, n = scales.shape
    words = np.ascontiguousarray(words).reshape(g, 128, n, -1)
    if fmt == "e4m3":
        vals = words.view(ml_dtypes.float8_e4m3fn).astype(np.float64)
    else:
        nib = np.empty((g, 128, n, 4), np.uint8)
        nib[..., 0::2] = words & 0xF
        nib[..., 1::2] = words >> 4
        vals = E2M1[nib]
    vals = vals * np.repeat(np.exp2(scales.astype(np.float64) - 127.0), 8, axis=1)[..., None]
    return vals.transpose(0, 1, 3, 2).reshape(g * 512, n)


D, K, T, U, I, Q = 512, 512, 1024, 1024, 512, 128


def setup_inputs():
    n = np.random.standard_normal
    idx = np.stack([np.random.permutation(T)[:I] for _ in range(8)])
    idx2 = np.stack([np.random.permutation(U)[:I] for _ in range(8)])
    idx3 = np.stack([np.random.permutation(U)[:I] for _ in range(8)])
    fd = mx_kscale(D)
    fk = mx_kscale(K)
    wqp = pack_weight(n((D, K)) * 1.0 / np.sqrt(D) * fd[:, None] * fk, "e4m3")
    keysp = pack_weight(n((K, T)) * 1.0 / np.sqrt(K) / fk[:, None], "e4m3")
    notesp = pack_weight(n((K, U)) * 1.0 / np.sqrt(K) / fk[:, None], "e2m1")
    return {
        "states": (n((D, Q)) * 0.95 / fd[:, None]).astype(np.float32),
        "wq_words": wqp[0],
        "wq_scales": wqp[1],
        "keys_words": keysp[0],
        "keys_scales": keysp[1],
        "notes_words": notesp[0],
        "notes_scales": notesp[1],
        "offs": striped8(idx),
        "offs2": striped8(idx2),
        "offs3": striped8(idx3),
    }


def reference(states, wq_words, wq_scales, keys_words, keys_scales, notes_words, notes_scales, offs, offs2, offs3):
    idx = unstriped8(offs)
    idx2 = unstriped8(offs2)
    idx3 = unstriped8(offs3)
    wqu = unpack_weight(wq_words, wq_scales, "e4m3")
    keysu = unpack_weight(keys_words, keys_scales, "e4m3")
    notesu = unpack_weight(notes_words, notes_scales, "e2m1")
    statesq = mxq(f64(states), 0, "e4m3")
    qv = wqu.T @ statesq
    qvq = mxq(qv, 0, "e4m3")
    a = qvq.T @ keysu
    b = qvq.T @ notesu
    f1 = np.zeros((Q, U))
    f1[np.arange(Q)[:, None], idx2[np.arange(Q) % 128 // 16]] = pick8(a, idx, 16)
    cc = b + f1
    y = pick8(cc, idx3, 16) - pick8(b, idx2, 16)
    return y

@@ -1,0 +1,198 @@
+from contextlib import ExitStack
+
+import concourse.mybir as mybir
+
+D, K, T, U, I, Q = 512, 512, 1024, 1024, 512, 128
+FLOPS = 2 * D * K * Q + 2 * K * Q * T + 2 * K * Q * U
+
+F32 = mybir.dt.float32
+BF16 = mybir.dt.bfloat16
+I32 = mybir.dt.int32
+U32 = mybir.dt.uint32
+U16 = mybir.dt.uint16
+U8 = mybir.dt.uint8
+FP8X4 = mybir.dt.float8_e4m3fn_x4
+FP4X4 = mybir.dt.float4_e2m1fn_x4
+COPY = mybir.ActivationFunctionType.Copy
+ADD = mybir.AluOpType.add
+SUBTRACT = mybir.AluOpType.subtract
+
+P = 128
+PACK = 4
+HALF = I // 2
+LIST_COLS = I // 16
+CAST_SPLIT = 88
+A_WIDTHS = (256, 256, 256, 128, 128)
+BANK = 512
+ADD_SPLIT = 768
+
+
+def load_scale_rows(queue, plane, scales, quadrants):
+    for quad in quadrants:
+        queue.dma_start(
+            out=plane[:].bitcast(I32)[32 * quad : 32 * quad + 4, :],
+            in_=scales[0].bitcast(I32)[4 * quad : 4 * quad + 4, :],
+        )
+
+
+def tile_attend_crossed_madetwo_kernel(
+    tc, states, wq_words, wq_scales, keys_words, keys_scales, notes_words, notes_scales, offs, offs2, offs3, out
+):
+    nc = tc.nc
+    with ExitStack() as ctx:
+        lists = ctx.enter_context(tc.tile_pool(name="lists", bufs=1))
+        sb = ctx.enter_context(tc.tile_pool(name="sb", bufs=1))
+        psum = ctx.enter_context(tc.psum_pool(name="psum", bufs=1))
+
+        idx = lists.tile([P, LIST_COLS], U16, name="idx")
+        idx2 = lists.tile([P, LIST_COLS], U16, name="idx2")
+        idx3 = lists.tile([P, LIST_COLS], U16, name="idx3")
+
+        wq_plane = sb.tile([P, K], U8, name="wq_plane", align_bytes=64)
+        keys_plane = sb.tile([P, T], U8, name="keys_plane", align_bytes=64)
+        notes_plane = sb.tile([P, U], U8, name="notes_plane", align_bytes=64)
+        f1 = sb.tile([P, U], F32, name="f1")
+        nc.vector.memset(wq_plane[:].bitcast(I32), 0)
+        nc.vector.memset(keys_plane[:].bitcast(I32), 0)
+        nc.vector.memset(notes_plane[:].bitcast(I32), 0)
+        nc.vector.memset(f1[:], 0.0)
+
+        states_raw = sb.tile([P, PACK, Q], F32, name="states_raw")
+        wq_codes = sb.tile([P, K], U32, name="wq_codes", align_bytes=64)
+        keys_codes = sb.tile([P, T], U32, name="keys_codes", align_bytes=64)
+        notes_codes = sb.tile([P, 2 * U], U8, name="notes_codes", align_bytes=64)
+
+        nc.sync.dma_start(out=states_raw[:], in_=states.rearrange("(p j) q -> p j q", j=PACK))
+        nc.sync.dma_start(
+            out=wq_codes[:].bitcast(I32), in_=wq_words[0].rearrange("p n t -> p (n t)").bitcast(I32)
+        )
+        load_scale_rows(nc.sync, wq_plane, wq_scales, range(4))
+        nc.sync.dma_start(
+            out=keys_codes[:].bitcast(I32), in_=keys_words[0].rearrange("p n t -> p (n t)").bitcast(I32)
+        )
+        load_scale_rows(nc.sync, keys_plane, keys_scales, range(4))
+        nc.sync.dma_start(idx[:], offs)
+        nc.sync.dma_start(idx2[:], offs2)
+        nc.sync.dma_start(out=notes_codes[:].bitcast(I32), in_=notes_words[0].bitcast(I32))
+        load_scale_rows(nc.sync, notes_plane, notes_scales, range(4))
+        nc.sync.dma_start(idx3[:], offs3)
+
+        states_bf = sb.tile([P, Q, PACK], BF16, name="states_bf", align_bytes=64)
+        nc.vector.tensor_copy(
+            out=states_bf[:, :CAST_SPLIT, :].rearrange("p (c i) j -> p c j i", i=4),
+            in_=states_raw[:, :, :CAST_SPLIT].rearrange("p j (c i) -> p c j i", i=4),
+        )
+        nc.scalar.activation(
+            states_bf[:, CAST_SPLIT:, :].rearrange("p (c i) j -> p c j i", i=4),
+            states_raw[:, :, CAST_SPLIT:].rearrange("p j (c i) -> p c j i", i=4),
+            COPY,
+        )
+
+        dealt_codes = [sb.tile([P, 2 * P], U32, name="dealt_codes%d" % h, align_bytes=64) for h in range(2)]
+        dealt_plane = [sb.tile([P, 2 * P], U8, name="dealt_plane%d" % h, align_bytes=64) for h in range(2)]
+
+        def deal_scales(h):
+            nc.vector.tensor_copy(
+                out=dealt_plane[h][:].rearrange("p (t m) -> p t m", t=2),
+                in_=wq_plane[:].rearrange("p (m t) -> p t m", t=PACK)[:, 2 * h : 2 * h + 2, :],
+            )
+
+        states_codes = sb.tile([P, Q], U32, name="states_codes", align_bytes=64)
+        states_plane = sb.tile([P, Q], U8, name="states_plane", align_bytes=64)
+        nc.vector.quantize_mx(
+            out=states_codes[:].bitcast(FP8X4),
+            scales=states_plane[:],
+            in_=states_bf[:].rearrange("p q j -> p (q j)"),
+        )
+        deal_scales(0)
+        deal_scales(1)
+        for h in range(2):
+            nc.scalar.copy(
+                out=dealt_codes[h][:].rearrange("p (t m) -> p m t", t=2),
+                in_=wq_codes[:].rearrange("p (m t) -> p m t", t=PACK)[:, :, 2 * h : 2 * h + 2],
+            )
+
+        qv_bf = sb.tile([P, Q, PACK], BF16, name="qv_bf", align_bytes=64)
+        for h in range(2):
+            qv_bank = psum.tile([P, 2, Q], F32, name="qv_bank%d" % h, tag="shared%d" % h)
+            for t in range(2):
+                cols = slice(t * P, (t + 1) * P)
+                nc.tensor.matmul_mx(
+                    out=qv_bank[:, t, :],
+                    lhsT=dealt_codes[h][:, cols].bitcast(FP8X4),
+                    lhsT_scale=dealt_plane[h][:, cols],
+                    rhs=states_codes[:].bitcast(FP8X4),
+                    rhs_scale=states_plane[:],
+                    start=True,
+                    stop=True,
+                )
+            pair_out = qv_bf[:, :, 2 * h : 2 * h + 2]
+            pair_in = qv_bank[:].rearrange("p t q -> p q t")
+            if h == 0:
+                nc.vector.tensor_copy(out=pair_out, in_=pair_in)
+            else:
+                nc.scalar.copy(out=pair_out, in_=pair_in)
+
+        qv_codes = sb.tile([P, Q], U32, name="qv_codes", align_bytes=64)
+        qv_plane = sb.tile([P, Q], U8, name="qv_plane", align_bytes=64)
+        nc.vector.quantize_mx(
+            out=qv_codes[:].bitcast(FP8X4), scales=qv_plane[:], in_=qv_bf[:].rearrange("p q j -> p (q j)")
+        )
+
+        a = sb.tile([P, T], F32, name="a")
+        start = 0
+        for piece, width in enumerate(A_WIDTHS):
+            cols = slice(start, start + width)
+            start = start + width
+            a_bank = psum.tile([P, width], F32, name="a_bank%d" % piece)
+            nc.tensor.matmul_mx(
+                out=a_bank[:],
+                lhsT=qv_codes[:].bitcast(FP8X4),
+                lhsT_scale=qv_plane[:],
+                rhs=keys_codes[:, cols].bitcast(FP8X4),
+                rhs_scale=keys_plane[:, cols],
+                start=True,
+                stop=True,
+            )
+            if piece % 2 == 0:
+                nc.scalar.copy(out=a[:, cols], in_=a_bank[:])
+            else:
+                nc.vector.tensor_copy(out=a[:, cols], in_=a_bank[:])
+
+        picked_a = sb.tile([P, I], F32, name="picked_a")
+        halves = [slice(h * LIST_COLS // 2, (h + 1) * LIST_COLS // 2) for h in range(2)]
+        nc.vector.tensor_copy(picked_a[:, :HALF], a[:].indirect(idx[:, halves[0]]))
+        nc.scalar.activation(picked_a[:, HALF:], a[:].indirect(idx[:, halves[1]]), COPY)
+        nc.vector.tensor_copy(f1[:].indirect(idx2[:]), picked_a[:])
+
+        b = sb.tile([P, U], F32, name="b")
+        b_banks = []
+        for h in range(2):
+            cols = slice(h * BANK, (h + 1) * BANK)
+            b_bank = psum.tile([P, BANK], F32, name="b_bank%d" % h, tag="shared%d" % h)
+            nc.tensor.matmul_mx(
+                out=b_bank[:],
+                lhsT=qv_codes[:].bitcast(FP8X4),
+                lhsT_scale=qv_plane[:],
+                rhs=notes_codes[:, 2 * h * BANK : 2 * (h + 1) * BANK].bitcast(FP4X4),
+                rhs_scale=notes_plane[:, cols],
+                start=True,
+                stop=True,
+            )
+            nc.scalar.copy(out=b[:, cols], in_=b_bank[:])
+            b_banks.append(b_bank)
+        picked_b = sb.tile([P, I], F32, name="picked_b")
+        nc.scalar.activation(picked_b[:], b[:].indirect(idx2[:]), COPY)
+
+        cc = sb.tile([P, U], F32, name="cc")
+        nc.vector.tensor_tensor(cc[:, :BANK], b_banks[0][:], f1[:, :BANK], ADD)
+        nc.vector.tensor_tensor(cc[:, BANK:ADD_SPLIT], b_banks[1][:, : ADD_SPLIT - BANK], f1[:, BANK:ADD_SPLIT], ADD)
+        nc.gpsimd.tensor_tensor(cc[:, ADD_SPLIT:], b[:, ADD_SPLIT:], f1[:, ADD_SPLIT:], ADD)
+
+        result = [sb.tile([P, HALF], F32, name="result%d" % h) for h in range(2)]
+        picked_cc = sb.tile([P, HALF], F32, name="picked_cc")
+        nc.vector.tensor_tensor(result[0][:], cc[:].indirect(idx3[:, halves[0]]), picked_b[:, :HALF], SUBTRACT)
+        nc.scalar.activation(picked_cc[:], cc[:].indirect(idx3[:, halves[1]]), COPY)
+        nc.sync.dma_start(out=out[:, :HALF], in_=result[0][:])
+        nc.vector.tensor_tensor(result[1][:], picked_cc[:], picked_b[:, HALF:], SUBTRACT)
+        nc.sync.dma_start(out=out[:, HALF:], in_=result[1][:])

@@ -133,6 +133,18 @@ def tile_attend_crossed_madetwo_kernel(
             else:
                 nc.scalar.copy(out=pair_out, in_=pair_in)
 
+        warm_bank = psum.tile([32, K], F32, name="warm_bank")
+        for warm in range(2):
+            nc.tensor.matmul_mx(
+                out=warm_bank[:],
+                lhsT=dealt_codes[1][:, :32].bitcast(FP8X4),
+                lhsT_scale=dealt_plane[1][:, :32],
+                rhs=wq_codes[:].bitcast(FP8X4),
+                rhs_scale=wq_plane[:],
+                start=True,
+                stop=True,
+            )
+
         qv_codes = sb.tile([P, Q], U32, name="qv_codes", align_bytes=64)
         qv_plane = sb.tile([P, Q], U8, name="qv_plane", align_bytes=64)
         nc.vector.quantize_mx(

@@ -22,9 +22,9 @@ PACK = 4
 HALF = I // 2
 LIST_COLS = I // 16
 CAST_SPLIT = 88
-A_WIDTHS = (256, 256, 256, 128, 128)
+A_WIDTHS = (128, 256, 256, 128, 128, 128)
 BANK = 512
-ADD_SPLIT = 768
+ADD_SPLIT = 704
 
 
 def load_scale_rows(queue, plane, scales, quadrants):
@@ -89,13 +89,7 @@ def tile_attend_crossed_madetwo_kernel(
         )
 
         dealt_codes = [sb.tile([P, 2 * P], U32, name="dealt_codes%d" % h, align_bytes=64) for h in range(2)]
-        dealt_plane = [sb.tile([P, 2 * P], U8, name="dealt_plane%d" % h, align_bytes=64) for h in range(2)]
-
-        def deal_scales(h):
-            nc.vector.tensor_copy(
-                out=dealt_plane[h][:].rearrange("p (t m) -> p t m", t=2),
-                in_=wq_plane[:].rearrange("p (m t) -> p t m", t=PACK)[:, 2 * h : 2 * h + 2, :],
-            )
+        dealt_plane = [sb.tile([P, P], U8, name="dealt_plane%d" % t, align_bytes=64) for t in range(PACK)]
 
         states_codes = sb.tile([P, Q], U32, name="states_codes", align_bytes=64)
         states_plane = sb.tile([P, Q], U8, name="states_plane", align_bytes=64)
@@ -104,8 +98,8 @@ def tile_attend_crossed_madetwo_kernel(
             scales=states_plane[:],
             in_=states_bf[:].rearrange("p q j -> p (q j)"),
         )
-        deal_scales(0)
-        deal_scales(1)
+        for t in range(PACK):
+            nc.vector.tensor_copy(out=dealt_plane[t][:], in_=wq_plane[:].rearrange("p (m t) -> p t m", t=PACK)[:, t, :])
         for h in range(2):
             nc.scalar.copy(
                 out=dealt_codes[h][:].rearrange("p (t m) -> p m t", t=2),
@@ -114,13 +108,13 @@ def tile_attend_crossed_madetwo_kernel(
 
         qv_bf = sb.tile([P, Q, PACK], BF16, name="qv_bf", align_bytes=64)
         for h in range(2):
-            qv_bank = psum.tile([P, 2, Q], F32, name="qv_bank%d" % h, tag="shared%d" % h)
+            qv_bank = psum.tile([P, 2, Q], F32, name="qv_bank%d" % h, tag="bank%d" % (4 + h))
             for t in range(2):
                 cols = slice(t * P, (t + 1) * P)
                 nc.tensor.matmul_mx(
                     out=qv_bank[:, t, :],
                     lhsT=dealt_codes[h][:, cols].bitcast(FP8X4),
-                    lhsT_scale=dealt_plane[h][:, cols],
+                    lhsT_scale=dealt_plane[2 * h + t][:],
                     rhs=states_codes[:].bitcast(FP8X4),
                     rhs_scale=states_plane[:],
                     start=True,
@@ -137,8 +131,8 @@ def tile_attend_crossed_madetwo_kernel(
         for warm in range(2):
             nc.tensor.matmul_mx(
                 out=warm_bank[:],
-                lhsT=dealt_codes[1][:, :32].bitcast(FP8X4),
-                lhsT_scale=dealt_plane[1][:, :32],
+                lhsT=dealt_codes[1][:, P : P + 32].bitcast(FP8X4),
+                lhsT_scale=dealt_plane[3][:, :32],
                 rhs=wq_codes[:].bitcast(FP8X4),
                 rhs_scale=wq_plane[:],
                 start=True,
@@ -156,7 +150,7 @@ def tile_attend_crossed_madetwo_kernel(
         for piece, width in enumerate(A_WIDTHS):
             cols = slice(start, start + width)
             start = start + width
-            a_bank = psum.tile([P, width], F32, name="a_bank%d" % piece)
+            a_bank = psum.tile([P, width], F32, name="a_bank%d" % piece, tag="bank%d" % piece)
             nc.tensor.matmul_mx(
                 out=a_bank[:],
                 lhsT=qv_codes[:].bitcast(FP8X4),
@@ -181,7 +175,7 @@ def tile_attend_crossed_madetwo_kernel(
         b_banks = []
         for h in range(2):
             cols = slice(h * BANK, (h + 1) * BANK)
-            b_bank = psum.tile([P, BANK], F32, name="b_bank%d" % h, tag="shared%d" % h)
+            b_bank = psum.tile([P, BANK], F32, name="b_bank%d" % h, tag="bank%d" % h)
             nc.tensor.matmul_mx(
                 out=b_bank[:],
                 lhsT=qv_codes[:].bitcast(FP8X4),
@@ -206,5 +200,8 @@ def tile_attend_crossed_madetwo_kernel(
         nc.vector.tensor_tensor(result[0][:], cc[:].indirect(idx3[:, halves[0]]), picked_b[:, :HALF], SUBTRACT)
         nc.scalar.activation(picked_cc[:], cc[:].indirect(idx3[:, halves[1]]), COPY)
         nc.sync.dma_start(out=out[:, :HALF], in_=result[0][:])
-        nc.vector.tensor_tensor(result[1][:], picked_cc[:], picked_b[:, HALF:], SUBTRACT)
-        nc.sync.dma_start(out=out[:, HALF:], in_=result[1][:])
+        for lo in (0, HALF // 2):
+            cols = slice(lo, lo + HALF // 2)
+            out_cols = slice(HALF + lo, HALF + lo + HALF // 2)
+            nc.vector.tensor_tensor(result[1][:, cols], picked_cc[:, cols], picked_b[:, out_cols], SUBTRACT)
+            nc.sync.dma_start(out=out[:, out_cols], in_=result[1][:, cols])

from contextlib import ExitStack

import concourse.mybir as mybir

D, K, T, U, I, Q = 512, 512, 1024, 1024, 512, 128
FLOPS = 2 * D * K * Q + 2 * K * Q * T + 2 * K * Q * U

F32 = mybir.dt.float32
BF16 = mybir.dt.bfloat16
I32 = mybir.dt.int32
U32 = mybir.dt.uint32
U16 = mybir.dt.uint16
U8 = mybir.dt.uint8
FP8X4 = mybir.dt.float8_e4m3fn_x4
FP4X4 = mybir.dt.float4_e2m1fn_x4
COPY = mybir.ActivationFunctionType.Copy
ADD = mybir.AluOpType.add
SUBTRACT = mybir.AluOpType.subtract

P = 128
PACK = 4
HALF = I // 2
LIST_COLS = I // 16
CAST_SPLIT = 88
A_WIDTHS = (128, 256, 256, 128, 128, 128)
BANK = 512
ADD_SPLIT = 704


def load_scale_rows(queue, plane, scales, quadrants):
    for quad in quadrants:
        queue.dma_start(
            out=plane[:].bitcast(I32)[32 * quad : 32 * quad + 4, :],
            in_=scales[0].bitcast(I32)[4 * quad : 4 * quad + 4, :],
        )


def tile_attend_crossed_madetwo_kernel(
    tc, states, wq_words, wq_scales, keys_words, keys_scales, notes_words, notes_scales, offs, offs2, offs3, out
):
    nc = tc.nc
    with ExitStack() as ctx:
        lists = ctx.enter_context(tc.tile_pool(name="lists", bufs=1))
        sb = ctx.enter_context(tc.tile_pool(name="sb", bufs=1))
        psum = ctx.enter_context(tc.psum_pool(name="psum", bufs=1))

        idx = lists.tile([P, LIST_COLS], U16, name="idx")
        idx2 = lists.tile([P, LIST_COLS], U16, name="idx2")
        idx3 = lists.tile([P, LIST_COLS], U16, name="idx3")

        wq_plane = sb.tile([P, K], U8, name="wq_plane", align_bytes=64)
        keys_plane = sb.tile([P, T], U8, name="keys_plane", align_bytes=64)
        notes_plane = sb.tile([P, U], U8, name="notes_plane", align_bytes=64)
        f1 = sb.tile([P, U], F32, name="f1")
        nc.vector.memset(wq_plane[:].bitcast(I32), 0)
        nc.vector.memset(keys_plane[:].bitcast(I32), 0)
        nc.vector.memset(notes_plane[:].bitcast(I32), 0)
        nc.vector.memset(f1[:], 0.0)

        states_raw = sb.tile([P, PACK, Q], F32, name="states_raw")
        wq_codes = sb.tile([P, K], U32, name="wq_codes", align_bytes=64)
        keys_codes = sb.tile([P, T], U32, name="keys_codes", align_bytes=64)
        notes_codes = sb.tile([P, 2 * U], U8, name="notes_codes", align_bytes=64)

        nc.sync.dma_start(out=states_raw[:], in_=states.rearrange("(p j) q -> p j q", j=PACK))
        nc.sync.dma_start(
            out=wq_codes[:].bitcast(I32), in_=wq_words[0].rearrange("p n t -> p (n t)").bitcast(I32)
        )
        load_scale_rows(nc.sync, wq_plane, wq_scales, range(4))
        nc.sync.dma_start(
            out=keys_codes[:].bitcast(I32), in_=keys_words[0].rearrange("p n t -> p (n t)").bitcast(I32)
        )
        load_scale_rows(nc.sync, keys_plane, keys_scales, range(4))
        nc.sync.dma_start(idx[:], offs)
        nc.sync.dma_start(idx2[:], offs2)
        nc.sync.dma_start(out=notes_codes[:].bitcast(I32), in_=notes_words[0].bitcast(I32))
        load_scale_rows(nc.sync, notes_plane, notes_scales, range(4))
        nc.sync.dma_start(idx3[:], offs3)

        states_bf = sb.tile([P, Q, PACK], BF16, name="states_bf", align_bytes=64)
        nc.vector.tensor_copy(
            out=states_bf[:, :CAST_SPLIT, :].rearrange("p (c i) j -> p c j i", i=4),
            in_=states_raw[:, :, :CAST_SPLIT].rearrange("p j (c i) -> p c j i", i=4),
        )
        nc.scalar.activation(
            states_bf[:, CAST_SPLIT:, :].rearrange("p (c i) j -> p c j i", i=4),
            states_raw[:, :, CAST_SPLIT:].rearrange("p j (c i) -> p c j i", i=4),
            COPY,
        )

        dealt_codes = [sb.tile([P, 2 * P], U32, name="dealt_codes%d" % h, align_bytes=64) for h in range(2)]
        dealt_plane = [sb.tile([P, P], U8, name="dealt_plane%d" % t, align_bytes=64) for t in range(PACK)]

        states_codes = sb.tile([P, Q], U32, name="states_codes", align_bytes=64)
        states_plane = sb.tile([P, Q], U8, name="states_plane", align_bytes=64)
        nc.vector.quantize_mx(
            out=states_codes[:].bitcast(FP8X4),
            scales=states_plane[:],
            in_=states_bf[:].rearrange("p q j -> p (q j)"),
        )
        for t in range(PACK):
            nc.vector.tensor_copy(out=dealt_plane[t][:], in_=wq_plane[:].rearrange("p (m t) -> p t m", t=PACK)[:, t, :])
        for h in range(2):
            nc.scalar.copy(
                out=dealt_codes[h][:].rearrange("p (t m) -> p m t", t=2),
                in_=wq_codes[:].rearrange("p (m t) -> p m t", t=PACK)[:, :, 2 * h : 2 * h + 2],
            )

        qv_bf = sb.tile([P, Q, PACK], BF16, name="qv_bf", align_bytes=64)
        for h in range(2):
            qv_bank = psum.tile([P, 2, Q], F32, name="qv_bank%d" % h, tag="bank%d" % (4 + h))
            for t in range(2):
                cols = slice(t * P, (t + 1) * P)
                nc.tensor.matmul_mx(
                    out=qv_bank[:, t, :],
                    lhsT=dealt_codes[h][:, cols].bitcast(FP8X4),
                    lhsT_scale=dealt_plane[2 * h + t][:],
                    rhs=states_codes[:].bitcast(FP8X4),
                    rhs_scale=states_plane[:],
                    start=True,
                    stop=True,
                )
            pair_out = qv_bf[:, :, 2 * h : 2 * h + 2]
            pair_in = qv_bank[:].rearrange("p t q -> p q t")
            if h == 0:
                nc.vector.tensor_copy(out=pair_out, in_=pair_in)
            else:
                nc.scalar.copy(out=pair_out, in_=pair_in)

        warm_bank = psum.tile([32, K], F32, name="warm_bank")
        for warm in range(2):
            nc.tensor.matmul_mx(
                out=warm_bank[:],
                lhsT=dealt_codes[1][:, P : P + 32].bitcast(FP8X4),
                lhsT_scale=dealt_plane[3][:, :32],
                rhs=wq_codes[:].bitcast(FP8X4),
                rhs_scale=wq_plane[:],
                start=True,
                stop=True,
            )

        qv_codes = sb.tile([P, Q], U32, name="qv_codes", align_bytes=64)
        qv_plane = sb.tile([P, Q], U8, name="qv_plane", align_bytes=64)
        nc.vector.quantize_mx(
            out=qv_codes[:].bitcast(FP8X4), scales=qv_plane[:], in_=qv_bf[:].rearrange("p q j -> p (q j)")
        )

        a = sb.tile([P, T], F32, name="a")
        start = 0
        for piece, width in enumerate(A_WIDTHS):
            cols = slice(start, start + width)
            start = start + width
            a_bank = psum.tile([P, width], F32, name="a_bank%d" % piece, tag="bank%d" % piece)
            nc.tensor.matmul_mx(
                out=a_bank[:],
                lhsT=qv_codes[:].bitcast(FP8X4),
                lhsT_scale=qv_plane[:],
                rhs=keys_codes[:, cols].bitcast(FP8X4),
                rhs_scale=keys_plane[:, cols],
                start=True,
                stop=True,
            )
            if piece % 2 == 0:
                nc.scalar.copy(out=a[:, cols], in_=a_bank[:])
            else:
                nc.vector.tensor_copy(out=a[:, cols], in_=a_bank[:])

        picked_a = sb.tile([P, I], F32, name="picked_a")
        halves = [slice(h * LIST_COLS // 2, (h + 1) * LIST_COLS // 2) for h in range(2)]
        nc.vector.tensor_copy(picked_a[:, :HALF], a[:].indirect(idx[:, halves[0]]))
        nc.scalar.activation(picked_a[:, HALF:], a[:].indirect(idx[:, halves[1]]), COPY)
        nc.vector.tensor_copy(f1[:].indirect(idx2[:]), picked_a[:])

        b = sb.tile([P, U], F32, name="b")
        b_banks = []
        for h in range(2):
            cols = slice(h * BANK, (h + 1) * BANK)
            b_bank = psum.tile([P, BANK], F32, name="b_bank%d" % h, tag="bank%d" % h)
            nc.tensor.matmul_mx(
                out=b_bank[:],
                lhsT=qv_codes[:].bitcast(FP8X4),
                lhsT_scale=qv_plane[:],
                rhs=notes_codes[:, 2 * h * BANK : 2 * (h + 1) * BANK].bitcast(FP4X4),
                rhs_scale=notes_plane[:, cols],
                start=True,
                stop=True,
            )
            nc.scalar.copy(out=b[:, cols], in_=b_bank[:])
            b_banks.append(b_bank)
        picked_b = sb.tile([P, I], F32, name="picked_b")
        nc.scalar.activation(picked_b[:], b[:].indirect(idx2[:]), COPY)

        cc = sb.tile([P, U], F32, name="cc")
        nc.vector.tensor_tensor(cc[:, :BANK], b_banks[0][:], f1[:, :BANK], ADD)
        nc.vector.tensor_tensor(cc[:, BANK:ADD_SPLIT], b_banks[1][:, : ADD_SPLIT - BANK], f1[:, BANK:ADD_SPLIT], ADD)
        nc.gpsimd.tensor_tensor(cc[:, ADD_SPLIT:], b[:, ADD_SPLIT:], f1[:, ADD_SPLIT:], ADD)

        result = [sb.tile([P, HALF], F32, name="result%d" % h) for h in range(2)]
        picked_cc = sb.tile([P, HALF], F32, name="picked_cc")
        nc.vector.tensor_tensor(result[0][:], cc[:].indirect(idx3[:, halves[0]]), picked_b[:, :HALF], SUBTRACT)
        nc.scalar.activation(picked_cc[:], cc[:].indirect(idx3[:, halves[1]]), COPY)
        nc.sync.dma_start(out=out[:, :HALF], in_=result[0][:])
        for lo in (0, HALF // 2):
            cols = slice(lo, lo + HALF // 2)
            out_cols = slice(HALF + lo, HALF + lo + HALF // 2)
            nc.vector.tensor_tensor(result[1][:, cols], picked_cc[:, cols], picked_b[:, out_cols], SUBTRACT)
            nc.sync.dma_start(out=out[:, out_cols], in_=result[1][:, cols])
